import numpy as np
import ml_dtypes


def mxq(x, axis, fmt="e4m3"):
    dtype, down = {"e4m3": (ml_dtypes.float8_e4m3fn, 7), "e5m2": (ml_dtypes.float8_e5m2, 14)}[fmt]
    v = np.moveaxis(np.asarray(x, np.float32).astype(ml_dtypes.bfloat16).astype(np.float64), axis, -1)
    blocks = v.reshape(v.shape[:-1] + (-1, 32))
    amax = np.abs(blocks).max(-1, keepdims=True)
    byte = np.maximum(np.where(amax > 0, np.frexp(amax)[1] - 1 + 127, 0) - down, 1)
    scale = np.exp2(byte - 127.0)
    codes = (blocks / scale).astype(np.float32).astype(dtype).astype(np.float64)
    return np.moveaxis((codes * scale).reshape(v.shape), -1, axis)


WIDE = False


def mx_kscale(k):
    if not WIDE:
        return np.ones(k)
    levels = np.array([10, -10, 5, -5, 0])
    if k % 512:
        return np.exp2(np.random.permutation(np.resize(levels, k // 32))).repeat(32)
    a = np.empty((k // 512, 16))
    for p in range(k // 512):
        a[p, :8] = np.random.permutation(np.resize(levels, 8))
        for g in range(8):
            far = levels[np.abs(levels - a[p, g]) >= 10]
            a[p, g + 8] = far[np.random.randint(len(far))]
    return np.exp2(a.ravel()).repeat(32)


def f64(x):
    return np.asarray(x).astype(np.float64)


def striped(idx):
    return np.tile(idx.reshape(-1, 16).T, (8, 1)).astype(np.uint16)


def unstriped(offs):
    return offs[:16].T.reshape(-1).astype(np.int64)


def striped8(idx):
    return np.concatenate([x.reshape(-1, 16).T for x in idx]).astype(np.uint16)


def runs(offs, k):
    lists = np.stack([offs[16 * r : 16 * r + 16].T.reshape(-1) for r in range(8)]).astype(np.int64)
    return lists[np.arange(k) % 512 // 64]


def pack_weight(w):
    k, n = w.shape
    w = f64(np.asarray(w, np.float32).astype(ml_dtypes.bfloat16)).reshape(k // 32, 32, n)
    amax = np.abs(w).max(1)
    byte = np.clip(np.where(amax > 0, np.frexp(amax)[1] - 1 + 127 - 7, 1), 1, 254)
    scaled = (w * np.exp2(127.0 - byte)[:, None, :]).reshape(k, n).astype(np.float32)
    words = np.ascontiguousarray(scaled.reshape(k // 512, 128, 4, n).transpose(0, 1, 3, 2)).astype(ml_dtypes.float8_e4m3fn).view(np.uint8)
    return words, np.ascontiguousarray(byte.astype(np.uint8).reshape(k // 512, 16, n))


def unpack_weight(words, scales):
    g, p, n, _ = words.shape
    vals = np.ascontiguousarray(words).view(ml_dtypes.float8_e4m3fn).astype(np.float64) * np.repeat(np.exp2(scales.astype(np.float64) - 127.0), 8, axis=1)[..., None]
    return vals.transpose(0, 1, 3, 2).reshape(g * 512, n)


E2M1 = np.array([0.0, 0.5, 1.0, 1.5, 2.0, 3.0, 4.0, 6.0, -0.0, -0.5, -1.0, -1.5, -2.0, -3.0, -4.0, -6.0])


def pack_fp4(w):
    k, n = w.shape
    w = f64(np.asarray(w, np.float32).astype(ml_dtypes.bfloat16)).reshape(k // 32, 32, n)
    amax = np.abs(w).max(1)
    mant, ex = np.frexp(amax / 6.0)
    byte = np.clip(np.where(amax > 0, np.where(mant > 0.5, ex, ex - 1) + 127, 1), 1, 254)
    scaled = (w * np.exp2(127.0 - byte)[:, None, :]).reshape(k, n).astype(np.float32)
    c = np.ascontiguousarray(scaled.reshape(k // 512, 128, 4, n).transpose(0, 1, 3, 2)).astype(ml_dtypes.float4_e2m1fn).view(np.uint8) & 0xF
    words = (c[..., 0::2] | (c[..., 1::2] << 4)).reshape(k // 512, 128, 2 * n)
    return np.ascontiguousarray(words), np.ascontiguousarray(byte.astype(np.uint8).reshape(k // 512, 16, n))


def unpack_fp4(words, scales):
    g, _, n = scales.shape
    words = np.ascontiguousarray(words).reshape(g, 128, n, 2)
    nib = np.empty((g, 128, n, 4), np.uint8)
    nib[..., 0::2] = words & 0xF
    nib[..., 1::2] = words >> 4
    vals = E2M1[nib] * np.repeat(np.exp2(scales.astype(np.float64) - 127.0), 8, axis=1)[..., None]
    return vals.transpose(0, 1, 3, 2).reshape(g * 512, n)


def planes(y):
    n, m = y.shape
    v = y.astype(np.float32).astype(ml_dtypes.bfloat16).astype(np.float64).reshape(n // 32, 32, m)
    top = np.abs(v).max(1)
    byte = np.clip(np.where(top > 0, np.frexp(top)[1] - 1 + 127 - 7, 1), 1, 254)
    codes = (v * np.exp2(127.0 - byte)[:, None, :]).reshape(n, m).astype(np.float32).astype(ml_dtypes.float8_e4m3fn).view(np.uint8)
    words = codes.reshape(n // 512, 128, 4, m).transpose(0, 1, 3, 2)
    return np.ascontiguousarray(words), np.ascontiguousarray(byte.astype(np.uint8).reshape(n // 512, 16, m))


K, T, S, N, G, H = 512, 2048, 512, 512, 2048, 512


def setup_inputs():
    n = np.random.standard_normal
    s = mx_kscale(K)[:, None]
    u = mx_kscale(H)
    packed_xT = pack_weight(n((K, T)) * s)
    packed_dT = pack_weight(n((K, G)) / s)
    packed_w1 = pack_fp4(n((H, N)) / np.sqrt(H) / u[:, None])
    return {
        "x_words": packed_xT[0],
        "x_scales": packed_xT[1],
        "d_words": packed_dT[0],
        "d_scales": packed_dT[1],
        "gn": (np.random.uniform(0.5, 1.5, (H, 1)) * u[:, None]).astype(np.float32),
        "w1_words": packed_w1[0],
        "w1_scales": packed_w1[1],
        "offs": striped(np.random.permutation(T)[:S]),
        "k1": striped8(np.random.randint(0, G, (8, H))),
        "k2": striped8(np.random.randint(0, G, (8, H))),
        "nb": striped8(np.stack([np.random.permutation(S) for _ in range(8)])),
    }


def reference(x_words, x_scales, d_words, d_scales, gn, w1_words, w1_scales, offs, k1, k2, nb):
    d_k1 = unpack_weight(d_words, d_scales)[np.arange(K)[:, None], runs(k1, K)]
    xq = unpack_weight(x_words, x_scales)[:, unstriped(offs)]
    a = 0.0625 * (d_k1.T @ xq)
    d_k2 = unpack_weight(d_words, d_scales)[np.arange(K)[:, None], runs(k2, K)]
    b = 0.0625 * (d_k2.T @ xq)
    z = f64(gn) * (a / (np.abs(b[np.arange(H)[:, None], runs(nb, H)]) + 0.5))
    out_0 = unpack_fp4(w1_words, w1_scales).T @ mxq(z, 0, "e4m3")
    return (out_0,) + planes(out_0)

@@ -1,0 +1,226 @@
+from contextlib import ExitStack
+
+import concourse.mybir as mybir
+
+K, T, S, N, G, H = 512, 2048, 512, 512, 2048, 512
+FLOPS = 2 * K * H * S * 2 + 2 * H * N * S
+
+F32 = mybir.dt.float32
+BF16 = mybir.dt.bfloat16
+I32 = mybir.dt.int32
+U32 = mybir.dt.uint32
+U16 = mybir.dt.uint16
+U8 = mybir.dt.uint8
+FP8X4 = mybir.dt.float8_e4m3fn_x4
+FP4X4 = mybir.dt.float4_e2m1fn_x4
+ACT = mybir.ActivationFunctionType
+ALU = mybir.AluOpType
+
+P = 128
+PACK = 4
+CHUNKS = ((0, 256), (256, 128), (384, 128))
+
+
+def tile_picked_scoredev2_none_po_kernel(
+    tc, x_words, x_scales, d_words, d_scales, gn, w1_words, w1_scales, offs, k1, k2, nb, out_0, out_1, out_2
+):
+    nc = tc.nc
+    with ExitStack() as ctx:
+        keep = ctx.enter_context(tc.tile_pool(name="keep", bufs=1))
+        psum = ctx.enter_context(tc.psum_pool(name="psum", bufs=1))
+
+        def tile(shape, dtype, name, tag=None):
+            return keep.tile(shape, dtype, name=name, tag=tag or name, align_bytes=64)
+
+        k2_l = tile([P, H // 16], U16, "k2_l")
+        offs_l = tile([P, S // 16], U16, "offs_l")
+        k1_l = tile([P, H // 16], U16, "k1_l")
+        nb_l = tile([P, S // 16], U16, "nb_l")
+
+        ds_win = tile([P, G], U8, "ds_win")
+        xs_win = tile([P, T], U8, "xs_win")
+        ws_raw = tile([P, N], U8, "ws_raw")
+        planes_b = tile([P, H + S], U8, "planes_b")
+        planes_a = tile([P, H + N], U8, "planes_a")
+        xw_win = tile([P, T], I32, "xw_win")
+        dw_win = tile([P, G], I32, "dw_win")
+        ww_raw = tile([P, 2 * N], U8, "ww_raw")
+        gn_sb = tile([P, PACK], F32, "gn_sb")
+
+        def spread_rows(rows):
+            words = rows[0].bitcast(I32)
+            return words.unsqueeze(1).to_broadcast([16, 8, words.shape[1]])
+
+        nc.sync.dma_start(k2_l[:], k2)
+        nc.sync.dma_start(ds_win[:].bitcast(I32), spread_rows(d_scales))
+        nc.sync.dma_start(offs_l[:], offs)
+        nc.sync.dma_start(xs_win[:].bitcast(I32), spread_rows(x_scales))
+        nc.sync.dma_start(dw_win[:], d_words[0].rearrange("p n t -> p (n t)").bitcast(I32))
+        nc.sync.dma_start(xw_win[:], x_words[0].rearrange("p n t -> p (n t)").bitcast(I32))
+        nc.sync.dma_start(k1_l[:], k1)
+        nc.sync.dma_start(nb_l[:], nb)
+        nc.gpsimd.dma_start(ws_raw[:].bitcast(I32), spread_rows(w1_scales))
+        nc.gpsimd.dma_start(gn_sb[:], gn.rearrange("(p t) o -> p (t o)", t=PACK))
+        nc.gpsimd.dma_start(ww_raw[:].bitcast(I32), w1_words[0].bitcast(I32))
+
+        nc.vector.memset(planes_b[:].bitcast(I32), 0)
+        nc.vector.memset(planes_a[:].bitcast(I32), 0)
+
+        def deal(dst, src):
+            nc.vector.tensor_copy(dst.rearrange("p (t m) -> p t m", t=PACK), src.rearrange("p (m t) -> p t m", t=PACK))
+
+        def place(queue, planes, spread):
+            for r in range(4):
+                queue.dma_start(planes[r:P:32, :].bitcast(I32), spread[8 * r : P : 32, :].bitcast(I32))
+
+        k2s_g = tile([P, H], U8, "k2s_g")
+        xs_g = tile([P, S], U8, "xs_g")
+        spread_b = tile([P, H + S], U8, "spread_b")
+        nc.vector.tensor_copy(k2s_g[:], ds_win[:].indirect(k2_l[:]))
+        nc.vector.tensor_copy(xs_g[:], xs_win[:].indirect(offs_l[:]))
+        deal(spread_b[:, 0:H], k2s_g[:])
+        nc.vector.tensor_copy(spread_b[:, H : H + S].bitcast(I32), xs_g[:].bitcast(I32))
+        place(nc.scalar, planes_b, spread_b)
+
+        k2w_g = tile([P, H], U32, "k2w_g")
+        k2w = tile([P, H], U32, "k2w")
+        nc.vector.tensor_copy(k2w_g[:], dw_win[:].bitcast(U32).indirect(k2_l[:]))
+        deal(k2w[:], k2w_g[:])
+        xw = tile([P, S], U32, "xw")
+        nc.vector.tensor_copy(xw[:], xw_win[:].bitcast(U32).indirect(offs_l[:]))
+
+        banks = [psum.tile([P, S], F32, name="bank%d" % i, tag="bank%d" % i) for i in range(PACK)]
+        a_ps = [psum.tile([P, S], F32, name="a_ps%d" % i) for i in range(PACK)]
+
+        def score(out, words, planes, t):
+            cols = slice(t * P, (t + 1) * P)
+            nc.tensor.matmul_mx(
+                out[:],
+                lhsT=words[:, cols].bitcast(FP8X4),
+                lhsT_scale=planes[:, cols],
+                rhs=xw[:].bitcast(FP8X4),
+                rhs_scale=planes_b[:, H : H + S],
+                start=True,
+                stop=True,
+            )
+
+        sizes = []
+        for t in range(PACK):
+            score(banks[t], k2w, planes_b, t)
+            size = tile([P, S], F32, "size%d" % t)
+            nc.scalar.activation(size[:], banks[t][:], ACT.Abs, scale=0.0625)
+            sizes.append(size)
+
+        k1s_g = tile([P, H], U8, "k1s_g", "xw_win")
+        spread_a = tile([P, H + N], U8, "spread_a", "k2w_g")
+        nc.vector.tensor_copy(k1s_g[:], ds_win[:].indirect(k1_l[:]))
+        deal(spread_a[:, H : H + N], ws_raw[:])
+        deal(spread_a[:, 0:H], k1s_g[:])
+        place(nc.sync, planes_a, spread_a)
+
+        recips = []
+
+        pieces = []
+
+        def fetch(c):
+            lo, width = CHUNKS[c]
+            rec = tile([P, PACK, width], F32, "rec%d" % c)
+            per_piece = S // width
+            for u in range(PACK // per_piece):
+                n = len(pieces)
+                fetched = tile([P, per_piece, width], F32, "fetched%d" % n, "fetched%d" % (n % 2))
+                root = tile([P, per_piece, width], F32, "root%d" % n)
+                pieces.append(fetched)
+                for v in range(per_piece):
+                    t = per_piece * u + v
+                    nc.vector.tensor_copy(fetched[:, v, :], sizes[t][:].indirect(nb_l[:, lo // 16 : (lo + width) // 16]))
+                nc.scalar.activation(root[:], fetched[:], ACT.Abs_reciprocal_sqrt, bias=0.5)
+                nc.scalar.activation(rec[:, per_piece * u : per_piece * (u + 1), :], root[:], ACT.Square, scale=0.25)
+            recips.append(rec)
+
+        fetch(0)
+        k1w_g = tile([P, H], U32, "k1w_g", "k2w")
+        k1w = tile([P, H], U32, "k1w")
+        nc.vector.tensor_copy(k1w_g[:], dw_win[:].bitcast(U32).indirect(k1_l[:]))
+        deal(k1w[:], k1w_g[:])
+        for t in range(PACK):
+            score(a_ps[t], k1w, planes_a, t)
+        ww = tile([P, 2 * N], U8, "ww", "k1w")
+        nc.vector.tensor_copy(
+            ww[:].rearrange("p (t m b) -> p t m b", t=PACK, b=2), ww_raw[:].rearrange("p (m t b) -> p t m b", t=PACK, b=2)
+        )
+
+        out_rows = out_0.rearrange("(p t) j -> p t j", t=PACK)
+        out_words = out_1[0].rearrange("p n t -> p (n t)").bitcast(I32)
+        y_scales = tile([P, S], U8, "y_scales")
+        groups = []
+        ys = []
+
+        def weigh(c):
+            lo, width = CHUNKS[c]
+            z_planes = tile([P, PACK, width], BF16, "z_planes%d" % c)
+            for t in range(PACK):
+                nc.vector.scalar_tensor_tensor(
+                    z_planes[:, t, :], a_ps[t][:, lo : lo + width], gn_sb[:, t : t + 1], recips[c][:, t, :], ALU.mult, ALU.mult
+                )
+            z_grouped = tile([P, width, PACK], BF16, "z_grouped%d" % c)
+            if c in (1, 2):
+                nc.vector.tensor_copy(z_grouped[:], z_planes[:].rearrange("p t j -> p j t"))
+            else:
+                nc.scalar.copy(z_grouped[:], z_planes[:].rearrange("p t j -> p j t"))
+            groups.append(z_grouped)
+
+        def project(c):
+            lo, width = CHUNKS[c]
+            z_codes = tile([P, width], U32, "z_codes%d" % c)
+            z_scales = tile([P, width], U8, "z_scales%d" % c)
+            nc.vector.quantize_mx(z_codes[:].bitcast(FP8X4), z_scales[:], groups[c][:].rearrange("p j t -> p (j t)"))
+            y = tile([P, PACK, width], F32, "y%d" % c)
+            per_bank = S // width
+            for u in range(PACK // per_bank):
+                slot = lo // P + u
+                bank = psum.tile([P, per_bank, width], F32, name="y_ps%d" % slot, tag="bank%d" % slot)
+                for v in range(per_bank):
+                    t = per_bank * u + v
+                    nc.tensor.matmul_mx(
+                        bank[:, v, :],
+                        lhsT=ww[:, 2 * t * P : 2 * (t + 1) * P].bitcast(FP4X4),
+                        lhsT_scale=planes_a[:, H + t * P : H + (t + 1) * P],
+                        rhs=z_codes[:].bitcast(FP8X4),
+                        rhs_scale=z_scales[:],
+                        start=True,
+                        stop=True,
+                    )
+                nc.scalar.copy(y[:, per_bank * u : per_bank * (u + 1), :], bank[:])
+            nc.sync.dma_start(out_rows[:, :, lo : lo + width], y[:])
+            ys.append(y)
+
+        def hand_on(c):
+            lo, width = CHUNKS[c]
+            y_grouped = tile([P, width, PACK], BF16, "y_grouped%d" % c)
+            if c in (0, 1, 2):
+                nc.vector.tensor_copy(y_grouped[:], ys[c][:].rearrange("p t j -> p j t"))
+            else:
+                nc.scalar.copy(y_grouped[:], ys[c][:].rearrange("p t j -> p j t"))
+            y_codes = tile([P, width], U32, "y_codes%d" % c)
+            nc.vector.quantize_mx(
+                y_codes[:].bitcast(FP8X4), y_scales[:, lo : lo + width], y_grouped[:].rearrange("p j t -> p (j t)")
+            )
+            nc.sync.dma_start(out_words[:, lo : lo + width], y_codes[:].bitcast(I32))
+
+        weigh(0)
+        fetch(1)
+        fetch(2)
+        project(0)
+        weigh(1)
+        weigh(2)
+        project(1)
+        hand_on(0)
+        project(2)
+        hand_on(1)
+        hand_on(2)
+
+        scale_rows = out_2[0].bitcast(I32)
+        for q in range(4):
+            queue = nc.sync if q % 2 == 0 else nc.scalar
+            queue.dma_start(scale_rows[4 * q : 4 * q + 4, :], y_scales[32 * q : 32 * q + 4, :].bitcast(I32))

@@ -39,52 +39,57 @@ def tile_picked_scoredev2_none_po_kernel(
 
         ds_win = tile([P, G], U8, "ds_win")
         xs_win = tile([P, T], U8, "xs_win")
-        ws_raw = tile([P, N], U8, "ws_raw")
-        planes_b = tile([P, H + S], U8, "planes_b")
-        planes_a = tile([P, H + N], U8, "planes_a")
+        rows_b = tile([P, H + S], U8, "rows_b")
+        rows_a = tile([P, H], U8, "rows_a")
         xw_win = tile([P, T], I32, "xw_win")
         dw_win = tile([P, G], I32, "dw_win")
         ww_raw = tile([P, 2 * N], U8, "ww_raw")
         gn_sb = tile([P, PACK], F32, "gn_sb")
 
-        def spread_rows(rows):
-            words = rows[0].bitcast(I32)
-            return words.unsqueeze(1).to_broadcast([16, 8, words.shape[1]])
-
+        nc.vector.memset(ds_win[:].bitcast(I32), 0)
+        nc.vector.memset(xs_win[:].bitcast(I32), 0)
+        nc.vector.memset(rows_b[:].bitcast(I32), 0)
+        nc.gpsimd.memset(rows_a[:].bitcast(I32), 0)
+        nc.sync.dma_start(ww_raw[:].bitcast(I32), w1_words[0].bitcast(I32))
         nc.sync.dma_start(k2_l[:], k2)
-        nc.sync.dma_start(ds_win[:].bitcast(I32), spread_rows(d_scales))
         nc.sync.dma_start(offs_l[:], offs)
-        nc.sync.dma_start(xs_win[:].bitcast(I32), spread_rows(x_scales))
-        nc.sync.dma_start(dw_win[:], d_words[0].rearrange("p n t -> p (n t)").bitcast(I32))
-        nc.sync.dma_start(xw_win[:], x_words[0].rearrange("p n t -> p (n t)").bitcast(I32))
         nc.sync.dma_start(k1_l[:], k1)
         nc.sync.dma_start(nb_l[:], nb)
-        nc.gpsimd.dma_start(ws_raw[:].bitcast(I32), spread_rows(w1_scales))
-        nc.gpsimd.dma_start(gn_sb[:], gn.rearrange("(p t) o -> p (t o)", t=PACK))
-        nc.gpsimd.dma_start(ww_raw[:].bitcast(I32), w1_words[0].bitcast(I32))
+        nc.sync.dma_start(gn_sb[:], gn.rearrange("(p t) o -> p (t o)", t=PACK))
+        nc.sync.dma_start(ds_win[0:P:8, :].bitcast(I32), d_scales[0].bitcast(I32))
+        nc.sync.dma_start(xs_win[0:P:8, :].bitcast(I32), x_scales[0].bitcast(I32))
+        nc.sync.dma_start(dw_win[:], d_words[0].rearrange("p n t -> p (n t)").bitcast(I32))
+        nc.sync.dma_start(xw_win[:], x_words[0].rearrange("p n t -> p (n t)").bitcast(I32))
+        for q in range(4):
+            nc.gpsimd.dma_start(rows_a[32 * q : 32 * q + 4, :].bitcast(I32), w1_scales[0].bitcast(I32)[4 * q : 4 * q + 4, :])
 
-        nc.vector.memset(planes_b[:].bitcast(I32), 0)
-        nc.vector.memset(planes_a[:].bitcast(I32), 0)
+
+        warm = tile([P, 1], F32, "warm")
+        warm_out = tile([P, 1], F32, "warm_out")
+        nc.vector.memset(warm[:], 1.0)
+        nc.scalar.activation(warm_out[:], warm[:], ACT.Abs_reciprocal_sqrt)
 
         def deal(dst, src):
             nc.vector.tensor_copy(dst.rearrange("p (t m) -> p t m", t=PACK), src.rearrange("p (m t) -> p t m", t=PACK))
 
-        def place(queue, planes, spread):
+        def place(queue, rows, first, spread):
             for r in range(4):
-                queue.dma_start(planes[r:P:32, :].bitcast(I32), spread[8 * r : P : 32, :].bitcast(I32))
+                queue.dma_start(rows[first + r : P : 32, :].bitcast(I32), spread[8 * r : P : 32, :].bitcast(I32))
 
-        k2s_g = tile([P, H], U8, "k2s_g")
-        xs_g = tile([P, S], U8, "xs_g")
-        spread_b = tile([P, H + S], U8, "spread_b")
-        nc.vector.tensor_copy(k2s_g[:], ds_win[:].indirect(k2_l[:]))
-        nc.vector.tensor_copy(xs_g[:], xs_win[:].indirect(offs_l[:]))
-        deal(spread_b[:, 0:H], k2s_g[:])
-        nc.vector.tensor_copy(spread_b[:, H : H + S].bitcast(I32), xs_g[:].bitcast(I32))
-        place(nc.scalar, planes_b, spread_b)
+        ww = tile([P, 2 * N], U8, "ww")
+        nc.vector.tensor_copy(
+            ww[:].rearrange("p (t m b) -> p t m b", t=PACK, b=2), ww_raw[:].rearrange("p (m t b) -> p t m b", t=PACK, b=2)
+        )
 
+        bs_g = tile([P, H + S], U8, "bs_g")
+        nc.vector.tensor_copy(bs_g[:, 0:H], ds_win[:].indirect(k2_l[:]))
+        nc.vector.tensor_copy(bs_g[:, H : H + S], xs_win[:].indirect(offs_l[:]))
+        place(nc.scalar, rows_b, 0, bs_g)
         k2w_g = tile([P, H], U32, "k2w_g")
         k2w = tile([P, H], U32, "k2w")
         nc.vector.tensor_copy(k2w_g[:], dw_win[:].bitcast(U32).indirect(k2_l[:]))
+        planes_b = tile([P, H], U8, "planes_b")
+        deal(planes_b[:], rows_b[:, 0:H])
         deal(k2w[:], k2w_g[:])
         xw = tile([P, S], U32, "xw")
         nc.vector.tensor_copy(xw[:], xw_win[:].bitcast(U32).indirect(offs_l[:]))
@@ -92,31 +97,28 @@ def tile_picked_scoredev2_none_po_kernel(
         banks = [psum.tile([P, S], F32, name="bank%d" % i, tag="bank%d" % i) for i in range(PACK)]
         a_ps = [psum.tile([P, S], F32, name="a_ps%d" % i) for i in range(PACK)]
 
-        def score(out, words, planes, t):
+        def score(out, words, planes, first, t):
             cols = slice(t * P, (t + 1) * P)
             nc.tensor.matmul_mx(
                 out[:],
                 lhsT=words[:, cols].bitcast(FP8X4),
-                lhsT_scale=planes[:, cols],
+                lhsT_scale=planes[first:P, cols],
                 rhs=xw[:].bitcast(FP8X4),
-                rhs_scale=planes_b[:, H : H + S],
+                rhs_scale=rows_b[:, H : H + S],
                 start=True,
                 stop=True,
             )
 
         sizes = []
         for t in range(PACK):
-            score(banks[t], k2w, planes_b, t)
+            score(banks[t], k2w, planes_b, 0, t)
             size = tile([P, S], F32, "size%d" % t)
             nc.scalar.activation(size[:], banks[t][:], ACT.Abs, scale=0.0625)
             sizes.append(size)
 
-        k1s_g = tile([P, H], U8, "k1s_g", "xw_win")
-        spread_a = tile([P, H + N], U8, "spread_a", "k2w_g")
+        k1s_g = tile([P, H], U8, "k1s_g", "xs_win")
         nc.vector.tensor_copy(k1s_g[:], ds_win[:].indirect(k1_l[:]))
-        deal(spread_a[:, H : H + N], ws_raw[:])
-        deal(spread_a[:, 0:H], k1s_g[:])
-        place(nc.sync, planes_a, spread_a)
+        place(nc.sync, rows_a, 4, k1s_g)
 
         recips = []
 
@@ -138,17 +140,19 @@ def tile_picked_scoredev2_none_po_kernel(
                 nc.scalar.activation(rec[:, per_piece * u : per_piece * (u + 1), :], root[:], ACT.Square, scale=0.25)
             recips.append(rec)
 
+        def score_a():
+            k1w_g = tile([P, H], U32, "k1w_g", "xw_win")
+            k1w = tile([P, H], U32, "k1w")
+            planes = tile([P, H], U8, "planes_a")
+            nc.vector.tensor_copy(k1w_g[:], dw_win[:].bitcast(U32).indirect(k1_l[:]))
+            deal(planes[:], rows_a[:])
+            deal(k1w[:], k1w_g[:])
+            for t in range(PACK):
+                score(a_ps[t], k1w, planes, 4, t)
+            return planes
+
+        planes_a = score_a()
         fetch(0)
-        k1w_g = tile([P, H], U32, "k1w_g", "k2w")
-        k1w = tile([P, H], U32, "k1w")
-        nc.vector.tensor_copy(k1w_g[:], dw_win[:].bitcast(U32).indirect(k1_l[:]))
-        deal(k1w[:], k1w_g[:])
-        for t in range(PACK):
-            score(a_ps[t], k1w, planes_a, t)
-        ww = tile([P, 2 * N], U8, "ww", "k1w")
-        nc.vector.tensor_copy(
-            ww[:].rearrange("p (t m b) -> p t m b", t=PACK, b=2), ww_raw[:].rearrange("p (m t b) -> p t m b", t=PACK, b=2)
-        )
 
         out_rows = out_0.rearrange("(p t) j -> p t j", t=PACK)
         out_words = out_1[0].rearrange("p n t -> p (n t)").bitcast(I32)
@@ -164,7 +168,7 @@ def tile_picked_scoredev2_none_po_kernel(
                     z_planes[:, t, :], a_ps[t][:, lo : lo + width], gn_sb[:, t : t + 1], recips[c][:, t, :], ALU.mult, ALU.mult
                 )
             z_grouped = tile([P, width, PACK], BF16, "z_grouped%d" % c)
-            if c in (1, 2):
+            if c in (2,):
                 nc.vector.tensor_copy(z_grouped[:], z_planes[:].rearrange("p t j -> p j t"))
             else:
                 nc.scalar.copy(z_grouped[:], z_planes[:].rearrange("p t j -> p j t"))
@@ -185,7 +189,7 @@ def tile_picked_scoredev2_none_po_kernel(
                     nc.tensor.matmul_mx(
                         bank[:, v, :],
                         lhsT=ww[:, 2 * t * P : 2 * (t + 1) * P].bitcast(FP4X4),
-                        lhsT_scale=planes_a[:, H + t * P : H + (t + 1) * P],
+                        lhsT_scale=planes_a[:, t * P : (t + 1) * P],
                         rhs=z_codes[:].bitcast(FP8X4),
                         rhs_scale=z_scales[:],
                         start=True,
@@ -198,7 +202,7 @@ def tile_picked_scoredev2_none_po_kernel(
         def hand_on(c):
             lo, width = CHUNKS[c]
             y_grouped = tile([P, width, PACK], BF16, "y_grouped%d" % c)
-            if c in (0, 1, 2):
+            if c in (1, 2):
                 nc.vector.tensor_copy(y_grouped[:], ys[c][:].rearrange("p t j -> p j t"))
             else:
                 nc.scalar.copy(y_grouped[:], ys[c][:].rearrange("p t j -> p j t"))
@@ -208,15 +212,15 @@ def tile_picked_scoredev2_none_po_kernel(
             )
             nc.sync.dma_start(out_words[:, lo : lo + width], y_codes[:].bitcast(I32))
 
-        weigh(0)
         fetch(1)
+        weigh(0)
         fetch(2)
         project(0)
         weigh(1)
         weigh(2)
         project(1)
-        hand_on(0)
         project(2)
+        hand_on(0)
         hand_on(1)
         hand_on(2)
 

@@ -18,7 +18,8 @@ ALU = mybir.AluOpType
 
 P = 128
 PACK = 4
-CHUNKS = ((0, 256), (256, 128), (384, 128))
+FETCH = ((0, 256), (256, 256))
+CHUNKS = ((0, 128), (128, 128), (256, 128), (384, 128))
 
 
 def tile_picked_scoredev2_none_po_kernel(
@@ -36,11 +37,9 @@ def tile_picked_scoredev2_none_po_kernel(
         offs_l = tile([P, S // 16], U16, "offs_l")
         k1_l = tile([P, H // 16], U16, "k1_l")
         nb_l = tile([P, S // 16], U16, "nb_l")
-
         ds_win = tile([P, G], U8, "ds_win")
         xs_win = tile([P, T], U8, "xs_win")
         rows_b = tile([P, H + S], U8, "rows_b")
-        rows_a = tile([P, H], U8, "rows_a")
         xw_win = tile([P, T], I32, "xw_win")
         dw_win = tile([P, G], I32, "dw_win")
         ww_raw = tile([P, 2 * N], U8, "ww_raw")
@@ -48,21 +47,19 @@ def tile_picked_scoredev2_none_po_kernel(
 
         nc.vector.memset(ds_win[:].bitcast(I32), 0)
         nc.vector.memset(xs_win[:].bitcast(I32), 0)
-        nc.vector.memset(rows_b[:].bitcast(I32), 0)
-        nc.gpsimd.memset(rows_a[:].bitcast(I32), 0)
+        nc.gpsimd.memset(rows_b[:].bitcast(I32), 0)
         nc.sync.dma_start(ww_raw[:].bitcast(I32), w1_words[0].bitcast(I32))
         nc.sync.dma_start(k2_l[:], k2)
         nc.sync.dma_start(offs_l[:], offs)
         nc.sync.dma_start(k1_l[:], k1)
         nc.sync.dma_start(nb_l[:], nb)
-        nc.sync.dma_start(gn_sb[:], gn.rearrange("(p t) o -> p (t o)", t=PACK))
         nc.sync.dma_start(ds_win[0:P:8, :].bitcast(I32), d_scales[0].bitcast(I32))
         nc.sync.dma_start(xs_win[0:P:8, :].bitcast(I32), x_scales[0].bitcast(I32))
         nc.sync.dma_start(dw_win[:], d_words[0].rearrange("p n t -> p (n t)").bitcast(I32))
         nc.sync.dma_start(xw_win[:], x_words[0].rearrange("p n t -> p (n t)").bitcast(I32))
         for q in range(4):
-            nc.gpsimd.dma_start(rows_a[32 * q : 32 * q + 4, :].bitcast(I32), w1_scales[0].bitcast(I32)[4 * q : 4 * q + 4, :])
-
+            nc.gpsimd.dma_start(rows_b[32 * q : 32 * q + 4, 0:H].bitcast(I32), w1_scales[0].bitcast(I32)[4 * q : 4 * q + 4, :])
+        nc.gpsimd.dma_start(gn_sb[:], gn.rearrange("(p t) o -> p (t o)", t=PACK))
 
         warm = tile([P, 1], F32, "warm")
         warm_out = tile([P, 1], F32, "warm_out")
@@ -71,6 +68,9 @@ def tile_picked_scoredev2_none_po_kernel(
 
         def deal(dst, src):
             nc.vector.tensor_copy(dst.rearrange("p (t m) -> p t m", t=PACK), src.rearrange("p (m t) -> p t m", t=PACK))
+
+        def deal_words(dst, src):
+            nc.vector.tensor_copy(dst.rearrange("p (t m) -> p m t", t=PACK), src.rearrange("p (m t) -> p m t", t=PACK))
 
         def place(queue, rows, first, spread):
             for r in range(4):
@@ -84,15 +84,18 @@ def tile_picked_scoredev2_none_po_kernel(
         bs_g = tile([P, H + S], U8, "bs_g")
         nc.vector.tensor_copy(bs_g[:, 0:H], ds_win[:].indirect(k2_l[:]))
         nc.vector.tensor_copy(bs_g[:, H : H + S], xs_win[:].indirect(offs_l[:]))
-        place(nc.scalar, rows_b, 0, bs_g)
+        place(nc.scalar, rows_b[:], 4, bs_g)
+        k1s_g = tile([P, H], U8, "k1s_g", "xs_win")
+        nc.vector.tensor_copy(k1s_g[:], ds_win[:].indirect(k1_l[:]))
+        place(nc.sync, rows_b[:, 0:H], 8, k1s_g)
         k2w_g = tile([P, H], U32, "k2w_g")
         k2w = tile([P, H], U32, "k2w")
         nc.vector.tensor_copy(k2w_g[:], dw_win[:].bitcast(U32).indirect(k2_l[:]))
         planes_b = tile([P, H], U8, "planes_b")
-        deal(planes_b[:], rows_b[:, 0:H])
-        deal(k2w[:], k2w_g[:])
         xw = tile([P, S], U32, "xw")
         nc.vector.tensor_copy(xw[:], xw_win[:].bitcast(U32).indirect(offs_l[:]))
+        deal_words(k2w[:], k2w_g[:])
+        deal(planes_b[:], rows_b[:, 0:H])
 
         banks = [psum.tile([P, S], F32, name="bank%d" % i, tag="bank%d" % i) for i in range(PACK)]
         a_ps = [psum.tile([P, S], F32, name="a_ps%d" % i) for i in range(PACK)]
@@ -104,33 +107,42 @@ def tile_picked_scoredev2_none_po_kernel(
                 lhsT=words[:, cols].bitcast(FP8X4),
                 lhsT_scale=planes[first:P, cols],
                 rhs=xw[:].bitcast(FP8X4),
-                rhs_scale=rows_b[:, H : H + S],
+                rhs_scale=rows_b[4:P, H : H + S],
                 start=True,
                 stop=True,
             )
 
         sizes = []
         for t in range(PACK):
-            score(banks[t], k2w, planes_b, 0, t)
+            score(banks[t], k2w, planes_b, 4, t)
             size = tile([P, S], F32, "size%d" % t)
             nc.scalar.activation(size[:], banks[t][:], ACT.Abs, scale=0.0625)
             sizes.append(size)
 
-        k1s_g = tile([P, H], U8, "k1s_g", "xs_win")
-        nc.vector.tensor_copy(k1s_g[:], ds_win[:].indirect(k1_l[:]))
-        place(nc.sync, rows_a, 4, k1s_g)
+
+        k1w_g = tile([P, H], U32, "k1w_g", "xs_win")
+        k1w = tile([P, H], U32, "k1w")
+        nc.vector.tensor_copy(k1w_g[:], dw_win[:].bitcast(U32).indirect(k1_l[:]))
+        deal_words(k1w[:], k1w_g[:])
+        for t in range(PACK):
+            score(a_ps[t], k1w, planes_b, 8, t)
 
         recips = []
-
         pieces = []
+        z_planes = []
+        groups = []
+        ys = []
+        out_rows = out_0.rearrange("(p t) j -> p t j", t=PACK)
+        out_words = out_1[0].rearrange("p n t -> p (n t)").bitcast(I32)
+        y_codes = tile([P, S], U32, "y_codes")
+        y_scales = tile([P, S], U8, "y_scales")
 
-        def fetch(c):
-            lo, width = CHUNKS[c]
-            rec = tile([P, PACK, width], F32, "rec%d" % c)
-            per_piece = S // width
+        def fetch(f, per_piece, tags):
+            lo, width = FETCH[f]
+            rec = tile([P, PACK, width], F32, "rec%d" % f)
             for u in range(PACK // per_piece):
                 n = len(pieces)
-                fetched = tile([P, per_piece, width], F32, "fetched%d" % n, "fetched%d" % (n % 2))
+                fetched = tile([P, per_piece, width], F32, "fetched%d" % n, tags[u])
                 root = tile([P, per_piece, width], F32, "root%d" % n)
                 pieces.append(fetched)
                 for v in range(per_piece):
@@ -140,38 +152,28 @@ def tile_picked_scoredev2_none_po_kernel(
                 nc.scalar.activation(rec[:, per_piece * u : per_piece * (u + 1), :], root[:], ACT.Square, scale=0.25)
             recips.append(rec)
 
-        def score_a():
-            k1w_g = tile([P, H], U32, "k1w_g", "xw_win")
-            k1w = tile([P, H], U32, "k1w")
-            planes = tile([P, H], U8, "planes_a")
-            nc.vector.tensor_copy(k1w_g[:], dw_win[:].bitcast(U32).indirect(k1_l[:]))
-            deal(planes[:], rows_a[:])
-            deal(k1w[:], k1w_g[:])
-            for t in range(PACK):
-                score(a_ps[t], k1w, planes, 4, t)
-            return planes
-
-        planes_a = score_a()
-        fetch(0)
-
-        out_rows = out_0.rearrange("(p t) j -> p t j", t=PACK)
-        out_words = out_1[0].rearrange("p n t -> p (n t)").bitcast(I32)
-        y_scales = tile([P, S], U8, "y_scales")
-        groups = []
-        ys = []
-
-        def weigh(c):
-            lo, width = CHUNKS[c]
-            z_planes = tile([P, PACK, width], BF16, "z_planes%d" % c)
+        def weigh(f):
+            lo, width = FETCH[f]
+            planes = tile([P, PACK, width], BF16, "z_planes%d" % f)
             for t in range(PACK):
                 nc.vector.scalar_tensor_tensor(
-                    z_planes[:, t, :], a_ps[t][:, lo : lo + width], gn_sb[:, t : t + 1], recips[c][:, t, :], ALU.mult, ALU.mult
+                    planes[:, t, :], a_ps[t][:, lo : lo + width], gn_sb[:, t : t + 1], recips[f][:, t, :], ALU.mult, ALU.mult
                 )
-            z_grouped = tile([P, width, PACK], BF16, "z_grouped%d" % c)
-            if c in (2,):
-                nc.vector.tensor_copy(z_grouped[:], z_planes[:].rearrange("p t j -> p j t"))
+            z_planes.append(planes)
+
+        def interleave(on_vector, dst, src):
+            dst = dst.rearrange("p (c i) t -> p c t i", i=4)
+            src = src.rearrange("p t (c i) -> p c t i", i=4)
+            if on_vector:
+                nc.vector.tensor_copy(dst, src)
             else:
-                nc.scalar.copy(z_grouped[:], z_planes[:].rearrange("p t j -> p j t"))
+                nc.scalar.copy(dst, src)
+
+        def group(c, f):
+            lo, width = CHUNKS[c]
+            at = lo - FETCH[f][0]
+            z_grouped = tile([P, width, PACK], BF16, "z_grouped%d" % c)
+            interleave(c in (2, 3), z_grouped[:], z_planes[f][:, :, at : at + width])
             groups.append(z_grouped)
 
         def project(c):
@@ -189,7 +191,7 @@ def tile_picked_scoredev2_none_po_kernel(
                     nc.tensor.matmul_mx(
                         bank[:, v, :],
                         lhsT=ww[:, 2 * t * P : 2 * (t + 1) * P].bitcast(FP4X4),
-                        lhsT_scale=planes_a[:, t * P : (t + 1) * P],
+                        lhsT_scale=planes_b[:, t * P : (t + 1) * P],
                         rhs=z_codes[:].bitcast(FP8X4),
                         rhs_scale=z_scales[:],
                         start=True,
@@ -202,28 +204,22 @@ def tile_picked_scoredev2_none_po_kernel(
         def hand_on(c):
             lo, width = CHUNKS[c]
             y_grouped = tile([P, width, PACK], BF16, "y_grouped%d" % c)
-            if c in (1, 2):
-                nc.vector.tensor_copy(y_grouped[:], ys[c][:].rearrange("p t j -> p j t"))
-            else:
-                nc.scalar.copy(y_grouped[:], ys[c][:].rearrange("p t j -> p j t"))
-            y_codes = tile([P, width], U32, "y_codes%d" % c)
+            interleave(c in (0, 1, 2, 3), y_grouped[:], ys[c][:])
             nc.vector.quantize_mx(
-                y_codes[:].bitcast(FP8X4), y_scales[:, lo : lo + width], y_grouped[:].rearrange("p j t -> p (j t)")
+                y_codes[:, lo : lo + width].bitcast(FP8X4), y_scales[:, lo : lo + width], y_grouped[:].rearrange("p j t -> p (j t)")
             )
-            nc.sync.dma_start(out_words[:, lo : lo + width], y_codes[:].bitcast(I32))
+            if c % 2 == 1:
+                half = slice(lo - width, lo + width)
+                nc.sync.dma_start(out_words[:, half], y_codes[:, half].bitcast(I32))
 
-        fetch(1)
+        fetch(0, 1, ("f0", "f1", "f2", "f3"))
+        fetch(1, 1, ("f0", "f1", "f2", "f3"))
         weigh(0)
-        fetch(2)
-        project(0)
         weigh(1)
-        weigh(2)
-        project(1)
-        project(2)
-        hand_on(0)
-        hand_on(1)
-        hand_on(2)
-
+        for c in range(4):
+            group(c, c // 2)
+            project(c)
+            hand_on(c)
         scale_rows = out_2[0].bitcast(I32)
         for q in range(4):
             queue = nc.sync if q % 2 == 0 else nc.scalar

from contextlib import ExitStack

import concourse.mybir as mybir

K, T, S, N, G, H = 512, 2048, 512, 512, 2048, 512
FLOPS = 2 * K * H * S * 2 + 2 * H * N * S

F32 = mybir.dt.float32
BF16 = mybir.dt.bfloat16
I32 = mybir.dt.int32
U32 = mybir.dt.uint32
U16 = mybir.dt.uint16
U8 = mybir.dt.uint8
FP8X4 = mybir.dt.float8_e4m3fn_x4
FP4X4 = mybir.dt.float4_e2m1fn_x4
ACT = mybir.ActivationFunctionType
ALU = mybir.AluOpType

P = 128
PACK = 4
FETCH = ((0, 256), (256, 256))
CHUNKS = ((0, 128), (128, 128), (256, 128), (384, 128))


def tile_picked_scoredev2_none_po_kernel(
    tc, x_words, x_scales, d_words, d_scales, gn, w1_words, w1_scales, offs, k1, k2, nb, out_0, out_1, out_2
):
    nc = tc.nc
    with ExitStack() as ctx:
        keep = ctx.enter_context(tc.tile_pool(name="keep", bufs=1))
        psum = ctx.enter_context(tc.psum_pool(name="psum", bufs=1))

        def tile(shape, dtype, name, tag=None):
            return keep.tile(shape, dtype, name=name, tag=tag or name, align_bytes=64)

        k2_l = tile([P, H // 16], U16, "k2_l")
        offs_l = tile([P, S // 16], U16, "offs_l")
        k1_l = tile([P, H // 16], U16, "k1_l")
        nb_l = tile([P, S // 16], U16, "nb_l")
        ds_win = tile([P, G], U8, "ds_win")
        xs_win = tile([P, T], U8, "xs_win")
        rows_b = tile([P, H + S], U8, "rows_b")
        xw_win = tile([P, T], I32, "xw_win")
        dw_win = tile([P, G], I32, "dw_win")
        ww_raw = tile([P, 2 * N], U8, "ww_raw")
        gn_sb = tile([P, PACK], F32, "gn_sb")

        nc.vector.memset(ds_win[:].bitcast(I32), 0)
        nc.vector.memset(xs_win[:].bitcast(I32), 0)
        nc.gpsimd.memset(rows_b[:].bitcast(I32), 0)
        nc.sync.dma_start(ww_raw[:].bitcast(I32), w1_words[0].bitcast(I32))
        nc.sync.dma_start(k2_l[:], k2)
        nc.sync.dma_start(offs_l[:], offs)
        nc.sync.dma_start(k1_l[:], k1)
        nc.sync.dma_start(nb_l[:], nb)
        nc.sync.dma_start(ds_win[0:P:8, :].bitcast(I32), d_scales[0].bitcast(I32))
        nc.sync.dma_start(xs_win[0:P:8, :].bitcast(I32), x_scales[0].bitcast(I32))
        nc.sync.dma_start(dw_win[:], d_words[0].rearrange("p n t -> p (n t)").bitcast(I32))
        nc.sync.dma_start(xw_win[:], x_words[0].rearrange("p n t -> p (n t)").bitcast(I32))
        for q in range(4):
            nc.gpsimd.dma_start(rows_b[32 * q : 32 * q + 4, 0:H].bitcast(I32), w1_scales[0].bitcast(I32)[4 * q : 4 * q + 4, :])
        nc.gpsimd.dma_start(gn_sb[:], gn.rearrange("(p t) o -> p (t o)", t=PACK))

        warm = tile([P, 1], F32, "warm")
        warm_out = tile([P, 1], F32, "warm_out")
        nc.vector.memset(warm[:], 1.0)
        nc.scalar.activation(warm_out[:], warm[:], ACT.Abs_reciprocal_sqrt)

        def deal(dst, src):
            nc.vector.tensor_copy(dst.rearrange("p (t m) -> p t m", t=PACK), src.rearrange("p (m t) -> p t m", t=PACK))

        def deal_words(dst, src):
            nc.vector.tensor_copy(dst.rearrange("p (t m) -> p m t", t=PACK), src.rearrange("p (m t) -> p m t", t=PACK))

        def place(queue, rows, first, spread):
            for r in range(4):
                queue.dma_start(rows[first + r : P : 32, :].bitcast(I32), spread[8 * r : P : 32, :].bitcast(I32))

        ww = tile([P, 2 * N], U8, "ww")
        nc.vector.tensor_copy(
            ww[:].rearrange("p (t m b) -> p t m b", t=PACK, b=2), ww_raw[:].rearrange("p (m t b) -> p t m b", t=PACK, b=2)
        )

        bs_g = tile([P, H + S], U8, "bs_g")
        nc.vector.tensor_copy(bs_g[:, 0:H], ds_win[:].indirect(k2_l[:]))
        nc.vector.tensor_copy(bs_g[:, H : H + S], xs_win[:].indirect(offs_l[:]))
        place(nc.scalar, rows_b[:], 4, bs_g)
        k1s_g = tile([P, H], U8, "k1s_g", "xs_win")
        nc.vector.tensor_copy(k1s_g[:], ds_win[:].indirect(k1_l[:]))
        place(nc.sync, rows_b[:, 0:H], 8, k1s_g)
        k2w_g = tile([P, H], U32, "k2w_g")
        k2w = tile([P, H], U32, "k2w")
        nc.vector.tensor_copy(k2w_g[:], dw_win[:].bitcast(U32).indirect(k2_l[:]))
        planes_b = tile([P, H], U8, "planes_b")
        xw = tile([P, S], U32, "xw")
        nc.vector.tensor_copy(xw[:], xw_win[:].bitcast(U32).indirect(offs_l[:]))
        deal_words(k2w[:], k2w_g[:])
        deal(planes_b[:], rows_b[:, 0:H])

        banks = [psum.tile([P, S], F32, name="bank%d" % i, tag="bank%d" % i) for i in range(PACK)]
        a_ps = [psum.tile([P, S], F32, name="a_ps%d" % i) for i in range(PACK)]

        def score(out, words, planes, first, t):
            cols = slice(t * P, (t + 1) * P)
            nc.tensor.matmul_mx(
                out[:],
                lhsT=words[:, cols].bitcast(FP8X4),
                lhsT_scale=planes[first:P, cols],
                rhs=xw[:].bitcast(FP8X4),
                rhs_scale=rows_b[4:P, H : H + S],
                start=True,
                stop=True,
            )

        sizes = []
        for t in range(PACK):
            score(banks[t], k2w, planes_b, 4, t)
            size = tile([P, S], F32, "size%d" % t)
            nc.scalar.activation(size[:], banks[t][:], ACT.Abs, scale=0.0625)
            sizes.append(size)


        k1w_g = tile([P, H], U32, "k1w_g", "xs_win")
        k1w = tile([P, H], U32, "k1w")
        nc.vector.tensor_copy(k1w_g[:], dw_win[:].bitcast(U32).indirect(k1_l[:]))
        deal_words(k1w[:], k1w_g[:])
        for t in range(PACK):
            score(a_ps[t], k1w, planes_b, 8, t)

        recips = []
        pieces = []
        z_planes = []
        groups = []
        ys = []
        out_rows = out_0.rearrange("(p t) j -> p t j", t=PACK)
        out_words = out_1[0].rearrange("p n t -> p (n t)").bitcast(I32)
        y_codes = tile([P, S], U32, "y_codes")
        y_scales = tile([P, S], U8, "y_scales")

        def fetch(f, per_piece, tags):
            lo, width = FETCH[f]
            rec = tile([P, PACK, width], F32, "rec%d" % f)
            for u in range(PACK // per_piece):
                n = len(pieces)
                fetched = tile([P, per_piece, width], F32, "fetched%d" % n, tags[u])
                root = tile([P, per_piece, width], F32, "root%d" % n)
                pieces.append(fetched)
                for v in range(per_piece):
                    t = per_piece * u + v
                    nc.vector.tensor_copy(fetched[:, v, :], sizes[t][:].indirect(nb_l[:, lo // 16 : (lo + width) // 16]))
                nc.scalar.activation(root[:], fetched[:], ACT.Abs_reciprocal_sqrt, bias=0.5)
                nc.scalar.activation(rec[:, per_piece * u : per_piece * (u + 1), :], root[:], ACT.Square, scale=0.25)
            recips.append(rec)

        def weigh(f):
            lo, width = FETCH[f]
            planes = tile([P, PACK, width], BF16, "z_planes%d" % f)
            for t in range(PACK):
                nc.vector.scalar_tensor_tensor(
                    planes[:, t, :], a_ps[t][:, lo : lo + width], gn_sb[:, t : t + 1], recips[f][:, t, :], ALU.mult, ALU.mult
                )
            z_planes.append(planes)

        def interleave(on_vector, dst, src):
            dst = dst.rearrange("p (c i) t -> p c t i", i=4)
            src = src.rearrange("p t (c i) -> p c t i", i=4)
            if on_vector:
                nc.vector.tensor_copy(dst, src)
            else:
                nc.scalar.copy(dst, src)

        def group(c, f):
            lo, width = CHUNKS[c]
            at = lo - FETCH[f][0]
            z_grouped = tile([P, width, PACK], BF16, "z_grouped%d" % c)
            interleave(c in (2, 3), z_grouped[:], z_planes[f][:, :, at : at + width])
            groups.append(z_grouped)

        def project(c):
            lo, width = CHUNKS[c]
            z_codes = tile([P, width], U32, "z_codes%d" % c)
            z_scales = tile([P, width], U8, "z_scales%d" % c)
            nc.vector.quantize_mx(z_codes[:].bitcast(FP8X4), z_scales[:], groups[c][:].rearrange("p j t -> p (j t)"))
            y = tile([P, PACK, width], F32, "y%d" % c)
            per_bank = S // width
            for u in range(PACK // per_bank):
                slot = lo // P + u
                bank = psum.tile([P, per_bank, width], F32, name="y_ps%d" % slot, tag="bank%d" % slot)
                for v in range(per_bank):
                    t = per_bank * u + v
                    nc.tensor.matmul_mx(
                        bank[:, v, :],
                        lhsT=ww[:, 2 * t * P : 2 * (t + 1) * P].bitcast(FP4X4),
                        lhsT_scale=planes_b[:, t * P : (t + 1) * P],
                        rhs=z_codes[:].bitcast(FP8X4),
                        rhs_scale=z_scales[:],
                        start=True,
                        stop=True,
                    )
                nc.scalar.copy(y[:, per_bank * u : per_bank * (u + 1), :], bank[:])
            nc.sync.dma_start(out_rows[:, :, lo : lo + width], y[:])
            ys.append(y)

        def hand_on(c):
            lo, width = CHUNKS[c]
            y_grouped = tile([P, width, PACK], BF16, "y_grouped%d" % c)
            interleave(c in (0, 1, 2, 3), y_grouped[:], ys[c][:])
            nc.vector.quantize_mx(
                y_codes[:, lo : lo + width].bitcast(FP8X4), y_scales[:, lo : lo + width], y_grouped[:].rearrange("p j t -> p (j t)")
            )
            if c % 2 == 1:
                half = slice(lo - width, lo + width)
                nc.sync.dma_start(out_words[:, half], y_codes[:, half].bitcast(I32))

        fetch(0, 1, ("f0", "f1", "f2", "f3"))
        fetch(1, 1, ("f0", "f1", "f2", "f3"))
        weigh(0)
        weigh(1)
        for c in range(4):
            group(c, c // 2)
            project(c)
            hand_on(c)
        scale_rows = out_2[0].bitcast(I32)
        for q in range(4):
            queue = nc.sync if q % 2 == 0 else nc.scalar
            queue.dma_start(scale_rows[4 * q : 4 * q + 4, :], y_scales[32 * q : 32 * q + 4, :].bitcast(I32))
